import numpy as np
import ml_dtypes


def mxq(x, axis, fmt="e4m3"):
    dtype, down = {"e4m3": (ml_dtypes.float8_e4m3fn, 7), "e5m2": (ml_dtypes.float8_e5m2, 14)}[fmt]
    v = np.moveaxis(np.asarray(x, np.float32).astype(ml_dtypes.bfloat16).astype(np.float64), axis, -1)
    blocks = v.reshape(v.shape[:-1] + (-1, 32))
    amax = np.abs(blocks).max(-1, keepdims=True)
    byte = np.maximum(np.where(amax > 0, np.frexp(amax)[1] - 1 + 127, 0) - down, 1)
    scale = np.exp2(byte - 127.0)
    codes = (blocks / scale).astype(np.float32).astype(dtype).astype(np.float64)
    return np.moveaxis((codes * scale).reshape(v.shape), -1, axis)


WIDE = False


def mx_kscale(k):
    if not WIDE:
        return np.ones(k)
    levels = np.array([10, -10, 5, -5, 0])
    if k % 512:
        return np.exp2(np.random.permutation(np.resize(levels, k // 32))).repeat(32)
    a = np.empty((k // 512, 16))
    for p in range(k // 512):
        a[p, :8] = np.random.permutation(np.resize(levels, 8))
        for g in range(8):
            far = levels[np.abs(levels - a[p, g]) >= 10]
            a[p, g + 8] = far[np.random.randint(len(far))]
    return np.exp2(a.ravel()).repeat(32)


def f64(x):
    return np.asarray(x).astype(np.float64)


def striped(idx):
    return np.tile(idx.reshape(-1, 16).T, (8, 1)).astype(np.uint16)


def unstriped(offs):
    return offs[:16].T.reshape(-1).astype(np.int64)


def striped8(idx):
    return np.concatenate([x.reshape(-1, 16).T for x in idx]).astype(np.uint16)


def runs(offs, k):
    lists = np.stack([offs[16 * r : 16 * r + 16].T.reshape(-1) for r in range(8)]).astype(np.int64)
    return lists[np.arange(k) % 512 // 64]


def pack_weight(w):
    k, n = w.shape
    w = f64(np.asarray(w, np.float32).astype(ml_dtypes.bfloat16)).reshape(k // 32, 32, n)
    amax = np.abs(w).max(1)
    byte = np.clip(np.where(amax > 0, np.frexp(amax)[1] - 1 + 127 - 7, 1), 1, 254)
    scaled = (w * np.exp2(127.0 - byte)[:, None, :]).reshape(k, n).astype(np.float32)
    words = np.ascontiguousarray(scaled.reshape(k // 512, 128, 4, n).transpose(0, 1, 3, 2)).astype(ml_dtypes.float8_e4m3fn).view(np.uint8)
    return words, np.ascontiguousarray(byte.astype(np.uint8).reshape(k // 512, 16, n))


def unpack_weight(words, scales):
    g, p, n, _ = words.shape
    vals = np.ascontiguousarray(words).view(ml_dtypes.float8_e4m3fn).astype(np.float64) * np.repeat(np.exp2(scales.astype(np.float64) - 127.0), 8, axis=1)[..., None]
    return vals.transpose(0, 1, 3, 2).reshape(g * 512, n)


K, T, S, N, G, H = 512, 1024, 512, 512, 2048, 512


def setup_inputs():
    n = np.random.standard_normal
    s = mx_kscale(K)[:, None]
    u = mx_kscale(S)
    packed_xT = pack_weight(n((K, T)) * s)
    packed_dT = pack_weight(n((K, G)) / s)
    return {
        "x_words": packed_xT[0],
        "x_scales": packed_xT[1],
        "d_words": packed_dT[0],
        "d_scales": packed_dT[1],
        "gn": (np.random.uniform(0.5, 1.5, (H, 1)) * u[:, None]).astype(np.float32),
        "gm": (np.random.uniform(0.5, 1.5, (H, 1)) * u[:, None]).astype(np.float32),
        "w1": (n((H, N)) / np.sqrt(2 * H) / u[:, None]).astype(np.float32),
        "w2": (n((H, N)) / np.sqrt(2 * H) / u[:, None]).astype(np.float32),
        "offs": striped(np.random.permutation(T)[:S]),
        "k1": striped8(np.random.randint(0, G, (8, H))),
        "two": striped(np.random.permutation(T)[:S]),
        "n1": striped8(np.stack([np.random.permutation(S) for _ in range(8)])),
        "n2": striped8(np.stack([np.random.permutation(S) for _ in range(8)])),
        "n3": striped8(np.stack([np.random.permutation(S) for _ in range(8)])),
        "n4": striped8(np.stack([np.random.permutation(S) for _ in range(8)])),
        "n5": striped(np.random.randint(0, S, G)),
    }


def reference(x_words, x_scales, d_words, d_scales, gn, gm, w1, w2, offs, k1, two, n1, n2, n3, n4, n5):
    d_k1 = unpack_weight(d_words, d_scales)[np.arange(K)[:, None], runs(k1, K)]
    xq = unpack_weight(x_words, x_scales)[:, unstriped(offs)]
    a = 0.0625 * (d_k1.T @ xq)
    z = f64(gn) * (a[np.arange(H)[:, None], runs(n1, H)] - (a[np.arange(H)[:, None], runs(n2, H)]))
    x_two = unpack_weight(x_words, x_scales)[:, unstriped(two)]
    b = 0.0625 * (d_k1.T @ x_two)
    ex = np.exp(b)
    z2 = f64(gm) * (np.log(ex + ex[np.arange(H)[:, None], runs(n3, H)]) - (b[np.arange(H)[:, None], runs(n4, H)]))
    h = mxq(f64(w1), 0, "e4m3").T @ mxq(z, 0, "e4m3") + mxq(f64(w2), 0, "e4m3").T @ mxq(z2, 0, "e4m3")
    mb = h[:, unstriped(n5)]
    mx = mb.reshape(N, S, 4).max(axis=2)
    mn = mb.reshape(N, S, 4).min(axis=2)
    return mx - (0.5 * mn)

@@ -1,0 +1,223 @@
+from contextlib import ExitStack
+
+import concourse.mybir as mybir
+from concourse.masks import make_identity
+
+F32 = mybir.dt.float32
+BF16 = mybir.dt.bfloat16
+I32 = mybir.dt.int32
+U32 = mybir.dt.uint32
+U16 = mybir.dt.uint16
+U8 = mybir.dt.uint8
+FP8X4 = mybir.dt.float8_e4m3fn_x4
+ALU = mybir.AluOpType
+ACT = mybir.ActivationFunctionType
+
+P = 128
+PACK = 4
+T, S, G = 1024, 512, 2048
+HALF = 256
+WINDOW = 1040
+PIECES = ((1024, 1024), (1024, 1024), (768, 704, 576), (512, 448, 416, 352, 320))
+FLOPS = 4 * 2 * 512 * 512 * 512
+
+
+def tile_picked_kjgaplsegspan_none_p_kernel(tc, x_words, x_scales, d_words, d_scales, gn, gm, w1, w2, offs, k1, two, n1, n2, n3, n4, n5, out):
+    nc = tc.nc
+    with ExitStack() as ctx:
+        lists = ctx.enter_context(tc.tile_pool(name="lists", bufs=1))
+        keep = ctx.enter_context(tc.tile_pool(name="keep", bufs=1))
+        ring = ctx.enter_context(tc.tile_pool(name="ring", bufs=2))
+        psum = ctx.enter_context(tc.psum_pool(name="psum", bufs=1))
+
+        def load_list(src, name):
+            tile = lists.tile(list(src.shape), U16, name=name)
+            nc.sync.dma_start(tile[:], src)
+            return tile
+
+        def half(lst, h):
+            return lst[:, 16 * h : 16 * (h + 1)]
+
+        d_bytes = keep.tile([P, G], U8, name="d_bytes", align_bytes=64)
+        x_bytes = keep.tile([P, T], U8, name="x_bytes", align_bytes=64)
+        key_scales = keep.tile([P, S], U8, name="key_scales", align_bytes=64)
+        nc.vector.memset(d_bytes[:].bitcast(I32), 0)
+        nc.vector.memset(x_bytes[:].bitcast(I32), 0)
+        nc.vector.memset(key_scales[:].bitcast(I32), 0)
+
+        k1_t = load_list(k1, "k1_t")
+        nc.scalar.dma_start(d_bytes[0:P:8, :].bitcast(I32), d_scales[0].bitcast(I32))
+        two_t = load_list(two, "two_t")
+        d_table = keep.tile([P, G], U32, name="d_table", tag="table_then_w1", align_bytes=64)
+        nc.sync.dma_start(d_table[:].bitcast(I32), d_words[0].rearrange("p n t -> p (n t)").bitcast(I32))
+        for q in range(4):
+            nc.gpsimd.dma_start(x_bytes[32 * q : 32 * q + 4, :].bitcast(I32), x_scales[0, 4 * q : 4 * q + 4, :].bitcast(I32))
+        gn_t = keep.tile([P, PACK], F32, name="gn_t")
+        gm_t = keep.tile([P, PACK], F32, name="gm_t")
+        nc.scalar.dma_start(gm_t[:], gm.rearrange("(p t) o -> p (t o)", t=PACK))
+        nc.scalar.dma_start(gn_t[:], gn.rearrange("(p t) o -> p (t o)", t=PACK))
+        offs_t = load_list(offs, "offs_t")
+        n3_t = load_list(n3, "n3_t")
+        n4_t = load_list(n4, "n4_t")
+        x_table = keep.tile([P, T], U32, name="x_table", align_bytes=64)
+        nc.sync.dma_start(x_table[:].bitcast(I32), x_words[0].rearrange("p n t -> p (n t)").bitcast(I32))
+        identity = keep.tile([P, P], F32, name="identity")
+        make_identity(nc, identity[:])
+        n2_t = load_list(n2, "n2_t")
+        n1_t = load_list(n1, "n1_t")
+        n5_t = load_list(n5, "n5_t")
+
+        key_bytes = keep.tile([P, S], U8, name="key_bytes", tag="key_picks", align_bytes=64)
+        nc.vector.tensor_copy(key_bytes[:], d_bytes[:].indirect(k1_t[:]))
+        dealt_bytes = keep.tile([P, S], U8, name="dealt_bytes", tag="bytes_then_w2", align_bytes=64)
+        nc.vector.tensor_copy(dealt_bytes[:].rearrange("p (t m) -> p t m", t=PACK), key_bytes[:].rearrange("p (m t) -> p t m", t=PACK))
+        for q in range(4):
+            nc.scalar.dma_start(key_scales[32 * q : 32 * q + 4, :].bitcast(I32), dealt_bytes[32 * q : 32 * q + 32 : 8, :].bitcast(I32))
+
+        key_words = keep.tile([P, S], U32, name="key_words", tag="key_picks", align_bytes=64)
+        nc.vector.tensor_copy(key_words[:], d_table[:].indirect(k1_t[:]))
+        key_codes = keep.tile([P, S], U32, name="key_codes", align_bytes=64)
+        nc.vector.tensor_copy(key_codes[:].rearrange("p (t m) -> p t m", t=PACK), key_words[:].rearrange("p (m t) -> p t m", t=PACK))
+
+        w_raw = []
+        for w, tag in ((w1, "table_then_w1"), (w2, "bytes_then_w2")):
+            raw = keep.tile([P, PACK, S], F32, name="w_raw", tag=tag, align_bytes=64)
+            nc.sync.dma_start(raw[:], w.rearrange("(p t) n -> p t n", t=PACK))
+            w_raw.append(raw)
+
+        def entries(lst, cols):
+            return lst[:, cols.start // 16 : cols.stop // 16]
+
+        def scores(lst, name, banks, parts, then):
+            codes = keep.tile([P, S], U32, name=name + "_codes", tag="token_codes", align_bytes=64)
+            scales = keep.tile([P, S], U8, name=name + "_scales", align_bytes=64)
+            for cols in parts:
+                nc.vector.tensor_copy(codes[:, cols], x_table[:].indirect(entries(lst, cols)))
+                nc.vector.tensor_copy(scales[:, cols], x_bytes[:].indirect(entries(lst, cols)))
+                for t in range(PACK):
+                    keys = slice(P * t, P * (t + 1))
+                    nc.tensor.matmul_mx(out=banks[t][:, cols], lhsT=key_codes[:, keys].bitcast(FP8X4), lhsT_scale=key_scales[:, keys],
+                                        rhs=codes[:, cols].bitcast(FP8X4), rhs_scale=scales[:, cols], start=True, stop=True)
+                    then(t, cols)
+
+        def bank_tiles(name, tag):
+            return [psum.tile([P, S], F32, name="%s%d" % (name, t), tag="%s%d" % (tag, t)) for t in range(PACK)]
+
+        def interleaved(tile, cols):
+            return tile[:, cols, :].rearrange("p (c i) t -> p c t i", i=2)
+
+        def planes(tile, cols):
+            return tile[:, :, cols].rearrange("p t (c i) -> p c t i", i=2)
+
+        def quantise(grouped, cols, codes, scales):
+            nc.vector.quantize_mx(out=codes[:, cols].bitcast(FP8X4), scales=scales[:, cols], in_=grouped[:, cols, :].rearrange("p c t -> p (c t)"))
+
+        halves = [slice(HALF * h, HALF * (h + 1)) for h in range(2)]
+        whole = slice(0, S)
+        ex = [keep.tile([P, 2 * S], F32, name="ex%d" % t) for t in range(PACK)]
+        b_banks = bank_tiles("b_bank", "first")
+        a_banks = bank_tiles("a_bank", "second")
+        scores(two_t, "b", b_banks, halves, lambda t, cols: nc.scalar.activation(ex[t][:, cols], b_banks[t][:, cols], ACT.Exp, scale=0.0625))
+        scores(offs_t, "a", a_banks, [whole], lambda t, cols: None)
+
+        w_codes = [keep.tile([P, S], U32, name="w_codes%d" % i, align_bytes=64) for i in range(2)]
+        w_scales = [keep.tile([P, S], U8, name="w_scales%d" % i, align_bytes=64) for i in range(2)]
+        w_grouped = [keep.tile([P, S, PACK], BF16, name="w_grouped%d" % i, align_bytes=64) for i in range(2)]
+        for i in range(2):
+            nc.gpsimd.tensor_scalar(w_grouped[i][:], w_raw[i][:].rearrange("p t c -> p c t"), 1.0, 0.0, op0=ALU.mult, op1=ALU.add)
+
+        a_rows = [keep.tile([P, S], F32, name="a_rows%d" % t) for t in range(PACK)]
+        b_rows = [keep.tile([P, 2 * S], F32, name="b_rows%d" % t) for t in range(PACK)]
+        for t in range(PACK):
+            nc.vector.tensor_scalar(b_rows[t][:, whole], b_banks[t][:], gm_t[:, t : t + 1], 0.0625, op0=ALU.mult, op1=ALU.mult)
+        for t in range(PACK):
+            nc.vector.tensor_scalar(a_rows[t][:], a_banks[t][:], gn_t[:, t : t + 1], 0.0625, op0=ALU.mult, op1=ALU.mult)
+
+        blocks = [slice(P * c, P * (c + 1)) for c in range(4)]
+        ex_n3 = keep.tile([P, PACK, S], F32, name="ex_n3")
+        sum_banks = bank_tiles("sum_bank", "first")
+        for t in range(PACK):
+            nc.scalar.activation(ex_n3[:, t, :], ex[t][:].indirect(n3_t[:]), ACT.Copy)
+            for c in range(4):
+                nc.tensor.matmul(sum_banks[t][:, blocks[c]], ex[t][:, blocks[c]], identity[:], start=(c == 0), stop=False, is_transpose=True)
+            for c in range(4):
+                nc.tensor.matmul(sum_banks[t][:, blocks[c]], ex_n3[:, t, blocks[c]], identity[:], start=False, stop=(c == 3), is_transpose=True)
+        for i in range(2):
+            quantise(w_grouped[i], whole, w_codes[i], w_scales[i])
+
+        a_n1 = keep.tile([P, PACK, S], F32, name="a_n1")
+        a_n2 = keep.tile([P, PACK, S], F32, name="a_n2")
+        b_n4 = keep.tile([P, PACK, S], F32, name="b_n4")
+        for h in range(2):
+            for t in range(PACK):
+                nc.vector.tensor_copy(a_n2[:, t, halves[h]], a_rows[t][:].indirect(entries(n2_t, halves[h])))
+        for t in range(2):
+            nc.scalar.activation(b_n4[:, t, :], b_rows[t][:].indirect(n4_t[:]), ACT.Copy)
+        logs_turned = keep.tile([P, PACK, S], F32, name="logs_turned")
+        log_banks = bank_tiles("log_bank", "second")
+        for t in range(PACK):
+            nc.scalar.activation(logs_turned[:, t, :], sum_banks[t][:], ACT.Ln)
+            for c in range(4):
+                nc.tensor.transpose(log_banks[t][:, blocks[c]], logs_turned[:, t, blocks[c]], identity[:])
+        for t in range(2, PACK):
+            nc.scalar.activation(b_n4[:, t, :], b_rows[t][:].indirect(n4_t[:]), ACT.Copy)
+
+        z_grouped = [keep.tile([P, S, PACK], BF16, name="z_grouped%d" % i, align_bytes=64) for i in range(2)]
+        z_codes = [keep.tile([P, S], U32, name="z_codes%d" % i, align_bytes=64) for i in range(2)]
+        z_scales = [keep.tile([P, S], U8, name="z_scales%d" % i, align_bytes=64) for i in range(2)]
+        z2 = keep.tile([P, PACK, S], F32, name="z2")
+        for t in range(PACK):
+            nc.vector.scalar_tensor_tensor(z2[:, t, :], log_banks[t][:], gm_t[:, t : t + 1], b_n4[:, t, :], op0=ALU.mult, op1=ALU.subtract)
+        nc.vector.tensor_copy(interleaved(z_grouped[1], whole), planes(z2, whole))
+        parts = [slice(0, 256), slice(256, 384), slice(384, 512)]
+        for cols in parts:
+            for t in range(PACK):
+                nc.scalar.activation(a_n1[:, t, cols], a_rows[t][:].indirect(entries(n1_t, cols)), ACT.Copy)
+            nc.vector.tensor_tensor(interleaved(z_grouped[0], cols), planes(a_n1, cols), planes(a_n2, cols), ALU.subtract)
+            if cols.start == 0:
+                quantise(z_grouped[1], whole, z_codes[1], z_scales[1])
+            quantise(z_grouped[0], cols, z_codes[0], z_scales[0])
+
+        h_rows = []
+        for m in range(4):
+            bank = psum.tile([P, S], F32, name="h_bank%d" % m, tag="first%d" % m)
+            cols = slice(P * m, P * (m + 1))
+            for i in (1, 0):
+                nc.tensor.matmul_mx(out=bank[:], lhsT=w_codes[i][:, cols].bitcast(FP8X4), lhsT_scale=w_scales[i][:, cols],
+                                    rhs=z_codes[i][:].bitcast(FP8X4), rhs_scale=z_scales[i][:], start=(i == 1), stop=(i == 0))
+            rows = keep.tile([P, WINDOW], F32, name="h_rows%d" % m)
+            if m == 0:
+                nc.scalar.copy(rows[:, 0:S], bank[:])
+            else:
+                nc.vector.tensor_copy(rows[:, 0:S], bank[:])
+            h_rows.append(rows)
+
+        pending = []
+
+        def finish():
+            m, cols, mx, mn = pending[0]
+            pending.clear()
+            width = cols.stop - cols.start
+            result = ring.tile([P, HALF], F32, name="result", bufs=3)
+            nc.vector.scalar_tensor_tensor(result[:, 0:width], mn[:, 0:width], -0.5, mx[:, 0:width], op0=ALU.mult, op1=ALU.add)
+            nc.sync.dma_start(out[P * m : P * (m + 1), cols], result[:, 0:width])
+
+        for m in range(4):
+            first = 0
+            for count in PIECES[m]:
+                width = count // 4
+                members = ring.tile([P, HALF, 4], F32, name="members", bufs=3)
+                nc.scalar.activation(members[:, 0:width, :].rearrange("p j t -> p (j t)"), h_rows[m][:].indirect(n5_t[:, first // 16 : (first + count) // 16]), ACT.Copy)
+                hi = ring.tile([P, HALF, 2], F32, name="hi")
+                lo = ring.tile([P, HALF, 2], F32, name="lo")
+                nc.vector.tensor_tensor(lo[:, 0:width, :], members[:, 0:width, 0:2], members[:, 0:width, 2:4], ALU.min)
+                nc.vector.tensor_tensor(hi[:, 0:width, :], members[:, 0:width, 0:2], members[:, 0:width, 2:4], ALU.max)
+                if pending:
+                    finish()
+                mx = ring.tile([P, HALF], F32, name="mx")
+                mn = ring.tile([P, HALF], F32, name="mn")
+                nc.vector.tensor_tensor(mn[:, 0:width], lo[:, 0:width, 0], lo[:, 0:width, 1], ALU.min)
+                nc.vector.tensor_tensor(mx[:, 0:width], hi[:, 0:width, 0], hi[:, 0:width, 1], ALU.max)
+                pending.append((m, slice(first // 4, first // 4 + width), mx, mn))
+                first = first + count
+        finish()

@@ -42,7 +42,7 @@ def tile_picked_kjgaplsegspan_none_p_kernel(tc, x_words, x_scales, d_words, d_sc
         x_bytes = keep.tile([P, T], U8, name="x_bytes", align_bytes=64)
         key_scales = keep.tile([P, S], U8, name="key_scales", align_bytes=64)
         nc.vector.memset(d_bytes[:].bitcast(I32), 0)
-        nc.vector.memset(x_bytes[:].bitcast(I32), 0)
+        nc.gpsimd.memset(x_bytes[:].bitcast(I32), 0)
         nc.vector.memset(key_scales[:].bitcast(I32), 0)
 
         k1_t = load_list(k1, "k1_t")
@@ -123,8 +123,6 @@ def tile_picked_kjgaplsegspan_none_p_kernel(tc, x_words, x_scales, d_words, d_sc
         w_codes = [keep.tile([P, S], U32, name="w_codes%d" % i, align_bytes=64) for i in range(2)]
         w_scales = [keep.tile([P, S], U8, name="w_scales%d" % i, align_bytes=64) for i in range(2)]
         w_grouped = [keep.tile([P, S, PACK], BF16, name="w_grouped%d" % i, align_bytes=64) for i in range(2)]
-        for i in range(2):
-            nc.gpsimd.tensor_scalar(w_grouped[i][:], w_raw[i][:].rearrange("p t c -> p c t"), 1.0, 0.0, op0=ALU.mult, op1=ALU.add)
 
         a_rows = [keep.tile([P, S], F32, name="a_rows%d" % t) for t in range(PACK)]
         b_rows = [keep.tile([P, 2 * S], F32, name="b_rows%d" % t) for t in range(PACK)]
@@ -142,6 +140,8 @@ def tile_picked_kjgaplsegspan_none_p_kernel(tc, x_words, x_scales, d_words, d_sc
                 nc.tensor.matmul(sum_banks[t][:, blocks[c]], ex[t][:, blocks[c]], identity[:], start=(c == 0), stop=False, is_transpose=True)
             for c in range(4):
                 nc.tensor.matmul(sum_banks[t][:, blocks[c]], ex_n3[:, t, blocks[c]], identity[:], start=False, stop=(c == 3), is_transpose=True)
+        for i in range(2):
+            nc.vector.tensor_copy(interleaved(w_grouped[i], whole), planes(w_raw[i], whole))
         for i in range(2):
             quantise(w_grouped[i], whole, w_codes[i], w_scales[i])
 
@@ -182,9 +182,10 @@ def tile_picked_kjgaplsegspan_none_p_kernel(tc, x_words, x_scales, d_words, d_sc
         for m in range(4):
             bank = psum.tile([P, S], F32, name="h_bank%d" % m, tag="first%d" % m)
             cols = slice(P * m, P * (m + 1))
-            for i in (1, 0):
-                nc.tensor.matmul_mx(out=bank[:], lhsT=w_codes[i][:, cols].bitcast(FP8X4), lhsT_scale=w_scales[i][:, cols],
-                                    rhs=z_codes[i][:].bitcast(FP8X4), rhs_scale=z_scales[i][:], start=(i == 1), stop=(i == 0))
+            passes = [(1, whole)] + [(0, part) for part in (parts if m == 0 else [whole])]
+            for n, (i, part) in enumerate(passes):
+                nc.tensor.matmul_mx(out=bank[:, part], lhsT=w_codes[i][:, cols].bitcast(FP8X4), lhsT_scale=w_scales[i][:, cols],
+                                    rhs=z_codes[i][:, part].bitcast(FP8X4), rhs_scale=z_scales[i][:, part], start=(n == 0), stop=(n == len(passes) - 1))
             rows = keep.tile([P, WINDOW], F32, name="h_rows%d" % m)
             if m == 0:
                 nc.scalar.copy(rows[:, 0:S], bank[:])

@@ -18,7 +18,7 @@ PACK = 4
 T, S, G = 1024, 512, 2048
 HALF = 256
 WINDOW = 1040
-PIECES = ((1024, 1024), (1024, 1024), (768, 704, 576), (512, 448, 416, 352, 320))
+PIECES = ((1024, 1024), (1024, 1024), (1024, 1024), (896, 672, 480))
 FLOPS = 4 * 2 * 512 * 512 * 512
 
 
@@ -42,32 +42,32 @@ def tile_picked_kjgaplsegspan_none_p_kernel(tc, x_words, x_scales, d_words, d_sc
         x_bytes = keep.tile([P, T], U8, name="x_bytes", align_bytes=64)
         key_scales = keep.tile([P, S], U8, name="key_scales", align_bytes=64)
         nc.vector.memset(d_bytes[:].bitcast(I32), 0)
-        nc.gpsimd.memset(x_bytes[:].bitcast(I32), 0)
+        nc.vector.memset(x_bytes[:].bitcast(I32), 0)
         nc.vector.memset(key_scales[:].bitcast(I32), 0)
 
         k1_t = load_list(k1, "k1_t")
         nc.scalar.dma_start(d_bytes[0:P:8, :].bitcast(I32), d_scales[0].bitcast(I32))
+        x_table = keep.tile([P, T], U32, name="x_table", align_bytes=64)
+        nc.sync.dma_start(x_table[:].bitcast(I32), x_words[0].rearrange("p n t -> p (n t)").bitcast(I32))
         two_t = load_list(two, "two_t")
+        offs_t = load_list(offs, "offs_t")
+        n3_t = load_list(n3, "n3_t")
         d_table = keep.tile([P, G], U32, name="d_table", tag="table_then_w1", align_bytes=64)
         nc.sync.dma_start(d_table[:].bitcast(I32), d_words[0].rearrange("p n t -> p (n t)").bitcast(I32))
         for q in range(4):
-            nc.gpsimd.dma_start(x_bytes[32 * q : 32 * q + 4, :].bitcast(I32), x_scales[0, 4 * q : 4 * q + 4, :].bitcast(I32))
+            nc.scalar.dma_start(x_bytes[32 * q : 32 * q + 4, :].bitcast(I32), x_scales[0, 4 * q : 4 * q + 4, :].bitcast(I32))
         gn_t = keep.tile([P, PACK], F32, name="gn_t")
         gm_t = keep.tile([P, PACK], F32, name="gm_t")
-        nc.scalar.dma_start(gm_t[:], gm.rearrange("(p t) o -> p (t o)", t=PACK))
-        nc.scalar.dma_start(gn_t[:], gn.rearrange("(p t) o -> p (t o)", t=PACK))
-        offs_t = load_list(offs, "offs_t")
-        n3_t = load_list(n3, "n3_t")
+        nc.gpsimd.dma_start(gm_t[:], gm.rearrange("(p t) o -> p (t o)", t=PACK))
+        nc.gpsimd.dma_start(gn_t[:], gn.rearrange("(p t) o -> p (t o)", t=PACK))
         n4_t = load_list(n4, "n4_t")
-        x_table = keep.tile([P, T], U32, name="x_table", align_bytes=64)
-        nc.sync.dma_start(x_table[:].bitcast(I32), x_words[0].rearrange("p n t -> p (n t)").bitcast(I32))
         identity = keep.tile([P, P], F32, name="identity")
         make_identity(nc, identity[:])
         n2_t = load_list(n2, "n2_t")
         n1_t = load_list(n1, "n1_t")
         n5_t = load_list(n5, "n5_t")
 
-        key_bytes = keep.tile([P, S], U8, name="key_bytes", tag="key_picks", align_bytes=64)
+        key_bytes = keep.tile([P, S], U8, name="key_bytes", tag="token_codes", align_bytes=64)
         nc.vector.tensor_copy(key_bytes[:], d_bytes[:].indirect(k1_t[:]))
         dealt_bytes = keep.tile([P, S], U8, name="dealt_bytes", tag="bytes_then_w2", align_bytes=64)
         nc.vector.tensor_copy(dealt_bytes[:].rearrange("p (t m) -> p t m", t=PACK), key_bytes[:].rearrange("p (m t) -> p t m", t=PACK))
@@ -88,9 +88,9 @@ def tile_picked_kjgaplsegspan_none_p_kernel(tc, x_words, x_scales, d_words, d_sc
         def entries(lst, cols):
             return lst[:, cols.start // 16 : cols.stop // 16]
 
-        def scores(lst, name, banks, parts, then):
+        def scores(lst, name, scale_tag, banks, parts, then):
             codes = keep.tile([P, S], U32, name=name + "_codes", tag="token_codes", align_bytes=64)
-            scales = keep.tile([P, S], U8, name=name + "_scales", align_bytes=64)
+            scales = keep.tile([P, S], U8, name=name + "_scales", tag=scale_tag, align_bytes=64)
             for cols in parts:
                 nc.vector.tensor_copy(codes[:, cols], x_table[:].indirect(entries(lst, cols)))
                 nc.vector.tensor_copy(scales[:, cols], x_bytes[:].indirect(entries(lst, cols)))
@@ -117,19 +117,17 @@ def tile_picked_kjgaplsegspan_none_p_kernel(tc, x_words, x_scales, d_words, d_sc
         ex = [keep.tile([P, 2 * S], F32, name="ex%d" % t) for t in range(PACK)]
         b_banks = bank_tiles("b_bank", "first")
         a_banks = bank_tiles("a_bank", "second")
-        scores(two_t, "b", b_banks, halves, lambda t, cols: nc.scalar.activation(ex[t][:, cols], b_banks[t][:, cols], ACT.Exp, scale=0.0625))
-        scores(offs_t, "a", a_banks, [whole], lambda t, cols: None)
+        scores(two_t, "b", "b_scales", b_banks, halves, lambda t, cols: nc.scalar.activation(ex[t][:, cols], b_banks[t][:, cols], ACT.Exp, scale=0.0625))
+        scores(offs_t, "a", "key_picks", a_banks, [whole], lambda t, cols: None)
 
-        w_codes = [keep.tile([P, S], U32, name="w_codes%d" % i, align_bytes=64) for i in range(2)]
-        w_scales = [keep.tile([P, S], U8, name="w_scales%d" % i, align_bytes=64) for i in range(2)]
-        w_grouped = [keep.tile([P, S, PACK], BF16, name="w_grouped%d" % i, align_bytes=64) for i in range(2)]
-
-        a_rows = [keep.tile([P, S], F32, name="a_rows%d" % t) for t in range(PACK)]
+        a_rows = [keep.tile([P, S], F32, name="a_rows%d" % t, align_bytes=64) for t in range(PACK)]
         b_rows = [keep.tile([P, 2 * S], F32, name="b_rows%d" % t) for t in range(PACK)]
         for t in range(PACK):
             nc.vector.tensor_scalar(b_rows[t][:, whole], b_banks[t][:], gm_t[:, t : t + 1], 0.0625, op0=ALU.mult, op1=ALU.mult)
-        for t in range(PACK):
+        for t in range(PACK - 1):
             nc.vector.tensor_scalar(a_rows[t][:], a_banks[t][:], gn_t[:, t : t + 1], 0.0625, op0=ALU.mult, op1=ALU.mult)
+        last_gain = keep.tile([P, 1], F32, name="last_gain")
+        nc.gpsimd.tensor_scalar(last_gain[:], gn_t[:, PACK - 1 : PACK], 0.0625, 0.0, op0=ALU.mult, op1=ALU.add)
 
         blocks = [slice(P * c, P * (c + 1)) for c in range(4)]
         ex_n3 = keep.tile([P, PACK, S], F32, name="ex_n3")
@@ -140,10 +138,13 @@ def tile_picked_kjgaplsegspan_none_p_kernel(tc, x_words, x_scales, d_words, d_sc
                 nc.tensor.matmul(sum_banks[t][:, blocks[c]], ex[t][:, blocks[c]], identity[:], start=(c == 0), stop=False, is_transpose=True)
             for c in range(4):
                 nc.tensor.matmul(sum_banks[t][:, blocks[c]], ex_n3[:, t, blocks[c]], identity[:], start=False, stop=(c == 3), is_transpose=True)
+        nc.scalar.activation(a_rows[PACK - 1][:], a_banks[PACK - 1][:], ACT.Copy, scale=last_gain[:])
+        head_grouped = keep.tile([P, 2 * P, PACK], BF16, name="head_grouped", align_bytes=64)
+        head_codes = keep.tile([P, 2 * P], U32, name="head_codes", align_bytes=64)
+        head_scales = keep.tile([P, 2 * P], U8, name="head_scales", align_bytes=64)
         for i in range(2):
-            nc.vector.tensor_copy(interleaved(w_grouped[i], whole), planes(w_raw[i], whole))
-        for i in range(2):
-            quantise(w_grouped[i], whole, w_codes[i], w_scales[i])
+            nc.vector.tensor_copy(interleaved(head_grouped, blocks[i]), planes(w_raw[i], blocks[0]))
+        quantise(head_grouped, halves[0], head_codes, head_scales)
 
         a_n1 = keep.tile([P, PACK, S], F32, name="a_n1")
         a_n2 = keep.tile([P, PACK, S], F32, name="a_n2")
@@ -151,6 +152,7 @@ def tile_picked_kjgaplsegspan_none_p_kernel(tc, x_words, x_scales, d_words, d_sc
         for h in range(2):
             for t in range(PACK):
                 nc.vector.tensor_copy(a_n2[:, t, halves[h]], a_rows[t][:].indirect(entries(n2_t, halves[h])))
+        nc.vector.tensor_copy(b_n4[:, 3, :], b_rows[3][:].indirect(n4_t[:]))
         for t in range(2):
             nc.scalar.activation(b_n4[:, t, :], b_rows[t][:].indirect(n4_t[:]), ACT.Copy)
         logs_turned = keep.tile([P, PACK, S], F32, name="logs_turned")
@@ -159,8 +161,7 @@ def tile_picked_kjgaplsegspan_none_p_kernel(tc, x_words, x_scales, d_words, d_sc
             nc.scalar.activation(logs_turned[:, t, :], sum_banks[t][:], ACT.Ln)
             for c in range(4):
                 nc.tensor.transpose(log_banks[t][:, blocks[c]], logs_turned[:, t, blocks[c]], identity[:])
-        for t in range(2, PACK):
-            nc.scalar.activation(b_n4[:, t, :], b_rows[t][:].indirect(n4_t[:]), ACT.Copy)
+        nc.scalar.activation(b_n4[:, 2, :], b_rows[2][:].indirect(n4_t[:]), ACT.Copy)
 
         z_grouped = [keep.tile([P, S, PACK], BF16, name="z_grouped%d" % i, align_bytes=64) for i in range(2)]
         z_codes = [keep.tile([P, S], U32, name="z_codes%d" % i, align_bytes=64) for i in range(2)]
@@ -178,13 +179,26 @@ def tile_picked_kjgaplsegspan_none_p_kernel(tc, x_words, x_scales, d_words, d_sc
                 quantise(z_grouped[1], whole, z_codes[1], z_scales[1])
             quantise(z_grouped[0], cols, z_codes[0], z_scales[0])
 
+        rest = slice(0, S - P)
+        rest_grouped = [keep.tile([P, S - P, PACK], BF16, name="rest_grouped%d" % i, tag=tag, align_bytes=64) for i, tag in enumerate(("a_rows3", "z_grouped0"))]
+        rest_codes = [keep.tile([P, S - P], U32, name="rest_codes%d" % i, align_bytes=64) for i in range(2)]
+        rest_scales = [keep.tile([P, S - P], U8, name="rest_scales%d" % i, align_bytes=64) for i in range(2)]
+        nc.scalar.copy(interleaved(rest_grouped[0], rest), planes(w_raw[0], slice(P, S)))
+        nc.vector.tensor_copy(interleaved(rest_grouped[1], rest), planes(w_raw[1], slice(P, S)))
+        for i in (1, 0):
+            quantise(rest_grouped[i], rest, rest_codes[i], rest_scales[i])
+
+        def weights(i, m):
+            if m == 0:
+                return head_codes[:, blocks[i]], head_scales[:, blocks[i]]
+            return rest_codes[i][:, blocks[m - 1]], rest_scales[i][:, blocks[m - 1]]
+
         h_rows = []
         for m in range(4):
             bank = psum.tile([P, S], F32, name="h_bank%d" % m, tag="first%d" % m)
-            cols = slice(P * m, P * (m + 1))
             passes = [(1, whole)] + [(0, part) for part in (parts if m == 0 else [whole])]
             for n, (i, part) in enumerate(passes):
-                nc.tensor.matmul_mx(out=bank[:, part], lhsT=w_codes[i][:, cols].bitcast(FP8X4), lhsT_scale=w_scales[i][:, cols],
+                nc.tensor.matmul_mx(out=bank[:, part], lhsT=weights(i, m)[0].bitcast(FP8X4), lhsT_scale=weights(i, m)[1],
                                     rhs=z_codes[i][:, part].bitcast(FP8X4), rhs_scale=z_scales[i][:, part], start=(n == 0), stop=(n == len(passes) - 1))
             rows = keep.tile([P, WINDOW], F32, name="h_rows%d" % m)
             if m == 0:
@@ -209,8 +223,8 @@ def tile_picked_kjgaplsegspan_none_p_kernel(tc, x_words, x_scales, d_words, d_sc
                 width = count // 4
                 members = ring.tile([P, HALF, 4], F32, name="members", bufs=3)
                 nc.scalar.activation(members[:, 0:width, :].rearrange("p j t -> p (j t)"), h_rows[m][:].indirect(n5_t[:, first // 16 : (first + count) // 16]), ACT.Copy)
-                hi = ring.tile([P, HALF, 2], F32, name="hi")
-                lo = ring.tile([P, HALF, 2], F32, name="lo")
+                hi = ring.tile([P, HALF, 2], F32, name="hi", bufs=1)
+                lo = ring.tile([P, HALF, 2], F32, name="lo", bufs=1)
                 nc.vector.tensor_tensor(lo[:, 0:width, :], members[:, 0:width, 0:2], members[:, 0:width, 2:4], ALU.min)
                 nc.vector.tensor_tensor(hi[:, 0:width, :], members[:, 0:width, 0:2], members[:, 0:width, 2:4], ALU.max)
                 if pending:

@@ -120,12 +120,12 @@ def tile_picked_kjgaplsegspan_none_p_kernel(tc, x_words, x_scales, d_words, d_sc
         scores(two_t, "b", "b_scales", b_banks, halves, lambda t, cols: nc.scalar.activation(ex[t][:, cols], b_banks[t][:, cols], ACT.Exp, scale=0.0625))
         scores(offs_t, "a", "key_picks", a_banks, [whole], lambda t, cols: None)
 
-        a_rows = [keep.tile([P, S], F32, name="a_rows%d" % t, align_bytes=64) for t in range(PACK)]
+        a_rows = [keep.tile([P, 2 * S], F32, name="a_rows%d" % t, align_bytes=64) for t in range(PACK)]
         b_rows = [keep.tile([P, 2 * S], F32, name="b_rows%d" % t) for t in range(PACK)]
         for t in range(PACK):
             nc.vector.tensor_scalar(b_rows[t][:, whole], b_banks[t][:], gm_t[:, t : t + 1], 0.0625, op0=ALU.mult, op1=ALU.mult)
         for t in range(PACK - 1):
-            nc.vector.tensor_scalar(a_rows[t][:], a_banks[t][:], gn_t[:, t : t + 1], 0.0625, op0=ALU.mult, op1=ALU.mult)
+            nc.vector.tensor_scalar(a_rows[t][:, whole], a_banks[t][:], gn_t[:, t : t + 1], 0.0625, op0=ALU.mult, op1=ALU.mult)
         last_gain = keep.tile([P, 1], F32, name="last_gain")
         nc.gpsimd.tensor_scalar(last_gain[:], gn_t[:, PACK - 1 : PACK], 0.0625, 0.0, op0=ALU.mult, op1=ALU.add)
 
@@ -138,7 +138,7 @@ def tile_picked_kjgaplsegspan_none_p_kernel(tc, x_words, x_scales, d_words, d_sc
                 nc.tensor.matmul(sum_banks[t][:, blocks[c]], ex[t][:, blocks[c]], identity[:], start=(c == 0), stop=False, is_transpose=True)
             for c in range(4):
                 nc.tensor.matmul(sum_banks[t][:, blocks[c]], ex_n3[:, t, blocks[c]], identity[:], start=False, stop=(c == 3), is_transpose=True)
-        nc.scalar.activation(a_rows[PACK - 1][:], a_banks[PACK - 1][:], ACT.Copy, scale=last_gain[:])
+        nc.scalar.activation(a_rows[PACK - 1][:, whole], a_banks[PACK - 1][:], ACT.Copy, scale=last_gain[:])
         head_grouped = keep.tile([P, 2 * P, PACK], BF16, name="head_grouped", align_bytes=64)
         head_codes = keep.tile([P, 2 * P], U32, name="head_codes", align_bytes=64)
         head_scales = keep.tile([P, 2 * P], U8, name="head_scales", align_bytes=64)
@@ -149,38 +149,45 @@ def tile_picked_kjgaplsegspan_none_p_kernel(tc, x_words, x_scales, d_words, d_sc
         a_n1 = keep.tile([P, PACK, S], F32, name="a_n1")
         a_n2 = keep.tile([P, PACK, S], F32, name="a_n2")
         b_n4 = keep.tile([P, PACK, S], F32, name="b_n4")
-        for h in range(2):
-            for t in range(PACK):
-                nc.vector.tensor_copy(a_n2[:, t, halves[h]], a_rows[t][:].indirect(entries(n2_t, halves[h])))
-        nc.vector.tensor_copy(b_n4[:, 3, :], b_rows[3][:].indirect(n4_t[:]))
-        for t in range(2):
-            nc.scalar.activation(b_n4[:, t, :], b_rows[t][:].indirect(n4_t[:]), ACT.Copy)
-        logs_turned = keep.tile([P, PACK, S], F32, name="logs_turned")
-        log_banks = bank_tiles("log_bank", "second")
-        for t in range(PACK):
-            nc.scalar.activation(logs_turned[:, t, :], sum_banks[t][:], ACT.Ln)
-            for c in range(4):
-                nc.tensor.transpose(log_banks[t][:, blocks[c]], logs_turned[:, t, blocks[c]], identity[:])
-        nc.scalar.activation(b_n4[:, 2, :], b_rows[2][:].indirect(n4_t[:]), ACT.Copy)
-
         z_grouped = [keep.tile([P, S, PACK], BF16, name="z_grouped%d" % i, align_bytes=64) for i in range(2)]
         z_codes = [keep.tile([P, S], U32, name="z_codes%d" % i, align_bytes=64) for i in range(2)]
         z_scales = [keep.tile([P, S], U8, name="z_scales%d" % i, align_bytes=64) for i in range(2)]
-        z2 = keep.tile([P, PACK, S], F32, name="z2")
-        for t in range(PACK):
-            nc.vector.scalar_tensor_tensor(z2[:, t, :], log_banks[t][:], gm_t[:, t : t + 1], b_n4[:, t, :], op0=ALU.mult, op1=ALU.subtract)
-        nc.vector.tensor_copy(interleaved(z_grouped[1], whole), planes(z2, whole))
-        parts = [slice(0, 256), slice(256, 384), slice(384, 512)]
-        for cols in parts:
+
+        def fetch_a_n1(cols):
             for t in range(PACK):
                 nc.scalar.activation(a_n1[:, t, cols], a_rows[t][:].indirect(entries(n1_t, cols)), ACT.Copy)
+
+        def make_z(cols):
             nc.vector.tensor_tensor(interleaved(z_grouped[0], cols), planes(a_n1, cols), planes(a_n2, cols), ALU.subtract)
-            if cols.start == 0:
-                quantise(z_grouped[1], whole, z_codes[1], z_scales[1])
-            quantise(z_grouped[0], cols, z_codes[0], z_scales[0])
+
+        fetch_a_n1(halves[0])
+        for t in range(PACK):
+            nc.vector.tensor_copy(a_n2[:, t, :], a_rows[t][:].indirect(n2_t[:]))
+        make_z(halves[0])
+        for t in range(2, PACK):
+            nc.vector.tensor_copy(b_n4[:, t, :], b_rows[t][:].indirect(n4_t[:]))
+        quantise(z_grouped[0], halves[0], z_codes[0], z_scales[0])
+        logs_turned = keep.tile([P, PACK, S], F32, name="logs_turned")
+        log_banks = bank_tiles("log_bank", "second")
+        for t in (2, 3, 0, 1):
+            nc.scalar.activation(logs_turned[:, t, :], sum_banks[t][:], ACT.Ln)
+            for c in range(4):
+                nc.tensor.transpose(log_banks[t][:, blocks[c]], logs_turned[:, t, blocks[c]], identity[:])
+        for t in range(2):
+            nc.scalar.activation(b_n4[:, t, :], b_rows[t][:].indirect(n4_t[:]), ACT.Copy)
+        z2 = keep.tile([P, PACK, S], F32, name="z2")
+        for t in (2, 3, 0, 1):
+            nc.vector.scalar_tensor_tensor(z2[:, t, :], log_banks[t][:], gm_t[:, t : t + 1], b_n4[:, t, :], op0=ALU.mult, op1=ALU.subtract)
+        fetch_a_n1(halves[1])
+        nc.vector.tensor_copy(interleaved(z_grouped[1], halves[0]), planes(z2, halves[0]))
+        nc.scalar.copy(interleaved(z_grouped[1], halves[1]), planes(z2, halves[1]))
+        make_z(halves[1])
+        quantise(z_grouped[1], halves[0], z_codes[1], z_scales[1])
+        quantise(z_grouped[0], halves[1], z_codes[0], z_scales[0])
+        quantise(z_grouped[1], halves[1], z_codes[1], z_scales[1])
 
         rest = slice(0, S - P)
-        rest_grouped = [keep.tile([P, S - P, PACK], BF16, name="rest_grouped%d" % i, tag=tag, align_bytes=64) for i, tag in enumerate(("a_rows3", "z_grouped0"))]
+        rest_grouped = [keep.tile([P, S - P, PACK], BF16, name="rest_grouped%d" % i, tag=tag, align_bytes=64) for i, tag in enumerate(("a_rows3", "z_grouped1"))]
         rest_codes = [keep.tile([P, S - P], U32, name="rest_codes%d" % i, align_bytes=64) for i in range(2)]
         rest_scales = [keep.tile([P, S - P], U8, name="rest_scales%d" % i, align_bytes=64) for i in range(2)]
         nc.scalar.copy(interleaved(rest_grouped[0], rest), planes(w_raw[0], slice(P, S)))
@@ -196,7 +203,7 @@ def tile_picked_kjgaplsegspan_none_p_kernel(tc, x_words, x_scales, d_words, d_sc
         h_rows = []
         for m in range(4):
             bank = psum.tile([P, S], F32, name="h_bank%d" % m, tag="first%d" % m)
-            passes = [(1, whole)] + [(0, part) for part in (parts if m == 0 else [whole])]
+            passes = [(0, halves[0]), (1, halves[0]), (0, halves[1]), (1, halves[1])] if m == 0 else [(0, whole), (1, whole)]
             for n, (i, part) in enumerate(passes):
                 nc.tensor.matmul_mx(out=bank[:, part], lhsT=weights(i, m)[0].bitcast(FP8X4), lhsT_scale=weights(i, m)[1],
                                     rhs=z_codes[i][:, part].bitcast(FP8X4), rhs_scale=z_scales[i][:, part], start=(n == 0), stop=(n == len(passes) - 1))

@@ -186,33 +186,31 @@ def tile_picked_kjgaplsegspan_none_p_kernel(tc, x_words, x_scales, d_words, d_sc
         quantise(z_grouped[0], halves[1], z_codes[0], z_scales[0])
         quantise(z_grouped[1], halves[1], z_codes[1], z_scales[1])
 
+        h_rows = [keep.tile([P, WINDOW], F32, name="h_rows%d" % m) for m in range(4)]
+
+        def product(bank, w_codes, w_scales, cols):
+            for i in range(2):
+                nc.tensor.matmul_mx(out=bank[:, cols], lhsT=w_codes[i].bitcast(FP8X4), lhsT_scale=w_scales[i],
+                                    rhs=z_codes[i][:, cols].bitcast(FP8X4), rhs_scale=z_scales[i][:, cols], start=(i == 0), stop=(i == 1))
+
+        head_banks = [psum.tile([P, S], F32, name="head_bank%d" % h, tag=tag) for h, tag in enumerate(("second0", "first0"))]
+        for h in range(2):
+            product(head_banks[h], [head_codes[:, blocks[i]] for i in range(2)], [head_scales[:, blocks[i]] for i in range(2)], halves[h])
+        nc.vector.tensor_copy(h_rows[0][:, halves[0]], head_banks[0][:, halves[0]])
+
         rest = slice(0, S - P)
         rest_grouped = [keep.tile([P, S - P, PACK], BF16, name="rest_grouped%d" % i, tag=tag, align_bytes=64) for i, tag in enumerate(("a_rows3", "z_grouped1"))]
         rest_codes = [keep.tile([P, S - P], U32, name="rest_codes%d" % i, align_bytes=64) for i in range(2)]
         rest_scales = [keep.tile([P, S - P], U8, name="rest_scales%d" % i, align_bytes=64) for i in range(2)]
         nc.scalar.copy(interleaved(rest_grouped[0], rest), planes(w_raw[0], slice(P, S)))
+        nc.scalar.copy(h_rows[0][:, halves[1]], head_banks[1][:, halves[1]])
         nc.vector.tensor_copy(interleaved(rest_grouped[1], rest), planes(w_raw[1], slice(P, S)))
         for i in (1, 0):
             quantise(rest_grouped[i], rest, rest_codes[i], rest_scales[i])
-
-        def weights(i, m):
-            if m == 0:
-                return head_codes[:, blocks[i]], head_scales[:, blocks[i]]
-            return rest_codes[i][:, blocks[m - 1]], rest_scales[i][:, blocks[m - 1]]
-
-        h_rows = []
-        for m in range(4):
+        for m in range(1, 4):
             bank = psum.tile([P, S], F32, name="h_bank%d" % m, tag="first%d" % m)
-            passes = [(0, halves[0]), (1, halves[0]), (0, halves[1]), (1, halves[1])] if m == 0 else [(0, whole), (1, whole)]
-            for n, (i, part) in enumerate(passes):
-                nc.tensor.matmul_mx(out=bank[:, part], lhsT=weights(i, m)[0].bitcast(FP8X4), lhsT_scale=weights(i, m)[1],
-                                    rhs=z_codes[i][:, part].bitcast(FP8X4), rhs_scale=z_scales[i][:, part], start=(n == 0), stop=(n == len(passes) - 1))
-            rows = keep.tile([P, WINDOW], F32, name="h_rows%d" % m)
-            if m == 0:
-                nc.scalar.copy(rows[:, 0:S], bank[:])
-            else:
-                nc.vector.tensor_copy(rows[:, 0:S], bank[:])
-            h_rows.append(rows)
+            product(bank, [rest_codes[i][:, blocks[m - 1]] for i in range(2)], [rest_scales[i][:, blocks[m - 1]] for i in range(2)], whole)
+            nc.vector.tensor_copy(h_rows[m][:, whole], bank[:])
 
         pending = []
 

from contextlib import ExitStack

import concourse.mybir as mybir
from concourse.masks import make_identity

F32 = mybir.dt.float32
BF16 = mybir.dt.bfloat16
I32 = mybir.dt.int32
U32 = mybir.dt.uint32
U16 = mybir.dt.uint16
U8 = mybir.dt.uint8
FP8X4 = mybir.dt.float8_e4m3fn_x4
ALU = mybir.AluOpType
ACT = mybir.ActivationFunctionType

P = 128
PACK = 4
T, S, G = 1024, 512, 2048
HALF = 256
WINDOW = 1040
PIECES = ((1024, 1024), (1024, 1024), (1024, 1024), (896, 672, 480))
FLOPS = 4 * 2 * 512 * 512 * 512


def tile_picked_kjgaplsegspan_none_p_kernel(tc, x_words, x_scales, d_words, d_scales, gn, gm, w1, w2, offs, k1, two, n1, n2, n3, n4, n5, out):
    nc = tc.nc
    with ExitStack() as ctx:
        lists = ctx.enter_context(tc.tile_pool(name="lists", bufs=1))
        keep = ctx.enter_context(tc.tile_pool(name="keep", bufs=1))
        ring = ctx.enter_context(tc.tile_pool(name="ring", bufs=2))
        psum = ctx.enter_context(tc.psum_pool(name="psum", bufs=1))

        def load_list(src, name):
            tile = lists.tile(list(src.shape), U16, name=name)
            nc.sync.dma_start(tile[:], src)
            return tile

        def half(lst, h):
            return lst[:, 16 * h : 16 * (h + 1)]

        d_bytes = keep.tile([P, G], U8, name="d_bytes", align_bytes=64)
        x_bytes = keep.tile([P, T], U8, name="x_bytes", align_bytes=64)
        key_scales = keep.tile([P, S], U8, name="key_scales", align_bytes=64)
        nc.vector.memset(d_bytes[:].bitcast(I32), 0)
        nc.vector.memset(x_bytes[:].bitcast(I32), 0)
        nc.vector.memset(key_scales[:].bitcast(I32), 0)

        k1_t = load_list(k1, "k1_t")
        nc.scalar.dma_start(d_bytes[0:P:8, :].bitcast(I32), d_scales[0].bitcast(I32))
        x_table = keep.tile([P, T], U32, name="x_table", align_bytes=64)
        nc.sync.dma_start(x_table[:].bitcast(I32), x_words[0].rearrange("p n t -> p (n t)").bitcast(I32))
        two_t = load_list(two, "two_t")
        offs_t = load_list(offs, "offs_t")
        n3_t = load_list(n3, "n3_t")
        d_table = keep.tile([P, G], U32, name="d_table", tag="table_then_w1", align_bytes=64)
        nc.sync.dma_start(d_table[:].bitcast(I32), d_words[0].rearrange("p n t -> p (n t)").bitcast(I32))
        for q in range(4):
            nc.scalar.dma_start(x_bytes[32 * q : 32 * q + 4, :].bitcast(I32), x_scales[0, 4 * q : 4 * q + 4, :].bitcast(I32))
        gn_t = keep.tile([P, PACK], F32, name="gn_t")
        gm_t = keep.tile([P, PACK], F32, name="gm_t")
        nc.gpsimd.dma_start(gm_t[:], gm.rearrange("(p t) o -> p (t o)", t=PACK))
        nc.gpsimd.dma_start(gn_t[:], gn.rearrange("(p t) o -> p (t o)", t=PACK))
        n4_t = load_list(n4, "n4_t")
        identity = keep.tile([P, P], F32, name="identity")
        make_identity(nc, identity[:])
        n2_t = load_list(n2, "n2_t")
        n1_t = load_list(n1, "n1_t")
        n5_t = load_list(n5, "n5_t")

        key_bytes = keep.tile([P, S], U8, name="key_bytes", tag="token_codes", align_bytes=64)
        nc.vector.tensor_copy(key_bytes[:], d_bytes[:].indirect(k1_t[:]))
        dealt_bytes = keep.tile([P, S], U8, name="dealt_bytes", tag="bytes_then_w2", align_bytes=64)
        nc.vector.tensor_copy(dealt_bytes[:].rearrange("p (t m) -> p t m", t=PACK), key_bytes[:].rearrange("p (m t) -> p t m", t=PACK))
        for q in range(4):
            nc.scalar.dma_start(key_scales[32 * q : 32 * q + 4, :].bitcast(I32), dealt_bytes[32 * q : 32 * q + 32 : 8, :].bitcast(I32))

        key_words = keep.tile([P, S], U32, name="key_words", tag="key_picks", align_bytes=64)
        nc.vector.tensor_copy(key_words[:], d_table[:].indirect(k1_t[:]))
        key_codes = keep.tile([P, S], U32, name="key_codes", align_bytes=64)
        nc.vector.tensor_copy(key_codes[:].rearrange("p (t m) -> p t m", t=PACK), key_words[:].rearrange("p (m t) -> p t m", t=PACK))

        w_raw = []
        for w, tag in ((w1, "table_then_w1"), (w2, "bytes_then_w2")):
            raw = keep.tile([P, PACK, S], F32, name="w_raw", tag=tag, align_bytes=64)
            nc.sync.dma_start(raw[:], w.rearrange("(p t) n -> p t n", t=PACK))
            w_raw.append(raw)

        def entries(lst, cols):
            return lst[:, cols.start // 16 : cols.stop // 16]

        def scores(lst, name, scale_tag, banks, parts, then):
            codes = keep.tile([P, S], U32, name=name + "_codes", tag="token_codes", align_bytes=64)
            scales = keep.tile([P, S], U8, name=name + "_scales", tag=scale_tag, align_bytes=64)
            for cols in parts:
                nc.vector.tensor_copy(codes[:, cols], x_table[:].indirect(entries(lst, cols)))
                nc.vector.tensor_copy(scales[:, cols], x_bytes[:].indirect(entries(lst, cols)))
                for t in range(PACK):
                    keys = slice(P * t, P * (t + 1))
                    nc.tensor.matmul_mx(out=banks[t][:, cols], lhsT=key_codes[:, keys].bitcast(FP8X4), lhsT_scale=key_scales[:, keys],
                                        rhs=codes[:, cols].bitcast(FP8X4), rhs_scale=scales[:, cols], start=True, stop=True)
                    then(t, cols)

        def bank_tiles(name, tag):
            return [psum.tile([P, S], F32, name="%s%d" % (name, t), tag="%s%d" % (tag, t)) for t in range(PACK)]

        def interleaved(tile, cols):
            return tile[:, cols, :].rearrange("p (c i) t -> p c t i", i=2)

        def planes(tile, cols):
            return tile[:, :, cols].rearrange("p t (c i) -> p c t i", i=2)

        def quantise(grouped, cols, codes, scales):
            nc.vector.quantize_mx(out=codes[:, cols].bitcast(FP8X4), scales=scales[:, cols], in_=grouped[:, cols, :].rearrange("p c t -> p (c t)"))

        halves = [slice(HALF * h, HALF * (h + 1)) for h in range(2)]
        whole = slice(0, S)
        ex = [keep.tile([P, 2 * S], F32, name="ex%d" % t) for t in range(PACK)]
        b_banks = bank_tiles("b_bank", "first")
        a_banks = bank_tiles("a_bank", "second")
        scores(two_t, "b", "b_scales", b_banks, halves, lambda t, cols: nc.scalar.activation(ex[t][:, cols], b_banks[t][:, cols], ACT.Exp, scale=0.0625))
        scores(offs_t, "a", "key_picks", a_banks, [whole], lambda t, cols: None)

        a_rows = [keep.tile([P, 2 * S], F32, name="a_rows%d" % t, align_bytes=64) for t in range(PACK)]
        b_rows = [keep.tile([P, 2 * S], F32, name="b_rows%d" % t) for t in range(PACK)]
        for t in range(PACK):
            nc.vector.tensor_scalar(b_rows[t][:, whole], b_banks[t][:], gm_t[:, t : t + 1], 0.0625, op0=ALU.mult, op1=ALU.mult)
        for t in range(PACK - 1):
            nc.vector.tensor_scalar(a_rows[t][:, whole], a_banks[t][:], gn_t[:, t : t + 1], 0.0625, op0=ALU.mult, op1=ALU.mult)
        last_gain = keep.tile([P, 1], F32, name="last_gain")
        nc.gpsimd.tensor_scalar(last_gain[:], gn_t[:, PACK - 1 : PACK], 0.0625, 0.0, op0=ALU.mult, op1=ALU.add)

        blocks = [slice(P * c, P * (c + 1)) for c in range(4)]
        ex_n3 = keep.tile([P, PACK, S], F32, name="ex_n3")
        sum_banks = bank_tiles("sum_bank", "first")
        for t in range(PACK):
            nc.scalar.activation(ex_n3[:, t, :], ex[t][:].indirect(n3_t[:]), ACT.Copy)
            for c in range(4):
                nc.tensor.matmul(sum_banks[t][:, blocks[c]], ex[t][:, blocks[c]], identity[:], start=(c == 0), stop=False, is_transpose=True)
            for c in range(4):
                nc.tensor.matmul(sum_banks[t][:, blocks[c]], ex_n3[:, t, blocks[c]], identity[:], start=False, stop=(c == 3), is_transpose=True)
        nc.scalar.activation(a_rows[PACK - 1][:, whole], a_banks[PACK - 1][:], ACT.Copy, scale=last_gain[:])
        head_grouped = keep.tile([P, 2 * P, PACK], BF16, name="head_grouped", align_bytes=64)
        head_codes = keep.tile([P, 2 * P], U32, name="head_codes", align_bytes=64)
        head_scales = keep.tile([P, 2 * P], U8, name="head_scales", align_bytes=64)
        for i in range(2):
            nc.vector.tensor_copy(interleaved(head_grouped, blocks[i]), planes(w_raw[i], blocks[0]))
        quantise(head_grouped, halves[0], head_codes, head_scales)

        a_n1 = keep.tile([P, PACK, S], F32, name="a_n1")
        a_n2 = keep.tile([P, PACK, S], F32, name="a_n2")
        b_n4 = keep.tile([P, PACK, S], F32, name="b_n4")
        z_grouped = [keep.tile([P, S, PACK], BF16, name="z_grouped%d" % i, align_bytes=64) for i in range(2)]
        z_codes = [keep.tile([P, S], U32, name="z_codes%d" % i, align_bytes=64) for i in range(2)]
        z_scales = [keep.tile([P, S], U8, name="z_scales%d" % i, align_bytes=64) for i in range(2)]

        def fetch_a_n1(cols):
            for t in range(PACK):
                nc.scalar.activation(a_n1[:, t, cols], a_rows[t][:].indirect(entries(n1_t, cols)), ACT.Copy)

        def make_z(cols):
            nc.vector.tensor_tensor(interleaved(z_grouped[0], cols), planes(a_n1, cols), planes(a_n2, cols), ALU.subtract)

        fetch_a_n1(halves[0])
        for t in range(PACK):
            nc.vector.tensor_copy(a_n2[:, t, :], a_rows[t][:].indirect(n2_t[:]))
        make_z(halves[0])
        for t in range(2, PACK):
            nc.vector.tensor_copy(b_n4[:, t, :], b_rows[t][:].indirect(n4_t[:]))
        quantise(z_grouped[0], halves[0], z_codes[0], z_scales[0])
        logs_turned = keep.tile([P, PACK, S], F32, name="logs_turned")
        log_banks = bank_tiles("log_bank", "second")
        for t in (2, 3, 0, 1):
            nc.scalar.activation(logs_turned[:, t, :], sum_banks[t][:], ACT.Ln)
            for c in range(4):
                nc.tensor.transpose(log_banks[t][:, blocks[c]], logs_turned[:, t, blocks[c]], identity[:])
        for t in range(2):
            nc.scalar.activation(b_n4[:, t, :], b_rows[t][:].indirect(n4_t[:]), ACT.Copy)
        z2 = keep.tile([P, PACK, S], F32, name="z2")
        for t in (2, 3, 0, 1):
            nc.vector.scalar_tensor_tensor(z2[:, t, :], log_banks[t][:], gm_t[:, t : t + 1], b_n4[:, t, :], op0=ALU.mult, op1=ALU.subtract)
        fetch_a_n1(halves[1])
        nc.vector.tensor_copy(interleaved(z_grouped[1], halves[0]), planes(z2, halves[0]))
        nc.scalar.copy(interleaved(z_grouped[1], halves[1]), planes(z2, halves[1]))
        make_z(halves[1])
        quantise(z_grouped[1], halves[0], z_codes[1], z_scales[1])
        quantise(z_grouped[0], halves[1], z_codes[0], z_scales[0])
        quantise(z_grouped[1], halves[1], z_codes[1], z_scales[1])

        h_rows = [keep.tile([P, WINDOW], F32, name="h_rows%d" % m) for m in range(4)]

        def product(bank, w_codes, w_scales, cols):
            for i in range(2):
                nc.tensor.matmul_mx(out=bank[:, cols], lhsT=w_codes[i].bitcast(FP8X4), lhsT_scale=w_scales[i],
                                    rhs=z_codes[i][:, cols].bitcast(FP8X4), rhs_scale=z_scales[i][:, cols], start=(i == 0), stop=(i == 1))

        head_banks = [psum.tile([P, S], F32, name="head_bank%d" % h, tag=tag) for h, tag in enumerate(("second0", "first0"))]
        for h in range(2):
            product(head_banks[h], [head_codes[:, blocks[i]] for i in range(2)], [head_scales[:, blocks[i]] for i in range(2)], halves[h])
        nc.vector.tensor_copy(h_rows[0][:, halves[0]], head_banks[0][:, halves[0]])

        rest = slice(0, S - P)
        rest_grouped = [keep.tile([P, S - P, PACK], BF16, name="rest_grouped%d" % i, tag=tag, align_bytes=64) for i, tag in enumerate(("a_rows3", "z_grouped1"))]
        rest_codes = [keep.tile([P, S - P], U32, name="rest_codes%d" % i, align_bytes=64) for i in range(2)]
        rest_scales = [keep.tile([P, S - P], U8, name="rest_scales%d" % i, align_bytes=64) for i in range(2)]
        nc.scalar.copy(interleaved(rest_grouped[0], rest), planes(w_raw[0], slice(P, S)))
        nc.scalar.copy(h_rows[0][:, halves[1]], head_banks[1][:, halves[1]])
        nc.vector.tensor_copy(interleaved(rest_grouped[1], rest), planes(w_raw[1], slice(P, S)))
        for i in (1, 0):
            quantise(rest_grouped[i], rest, rest_codes[i], rest_scales[i])
        for m in range(1, 4):
            bank = psum.tile([P, S], F32, name="h_bank%d" % m, tag="first%d" % m)
            product(bank, [rest_codes[i][:, blocks[m - 1]] for i in range(2)], [rest_scales[i][:, blocks[m - 1]] for i in range(2)], whole)
            nc.vector.tensor_copy(h_rows[m][:, whole], bank[:])

        pending = []

        def finish():
            m, cols, mx, mn = pending[0]
            pending.clear()
            width = cols.stop - cols.start
            result = ring.tile([P, HALF], F32, name="result", bufs=3)
            nc.vector.scalar_tensor_tensor(result[:, 0:width], mn[:, 0:width], -0.5, mx[:, 0:width], op0=ALU.mult, op1=ALU.add)
            nc.sync.dma_start(out[P * m : P * (m + 1), cols], result[:, 0:width])

        for m in range(4):
            first = 0
            for count in PIECES[m]:
                width = count // 4
                members = ring.tile([P, HALF, 4], F32, name="members", bufs=3)
                nc.scalar.activation(members[:, 0:width, :].rearrange("p j t -> p (j t)"), h_rows[m][:].indirect(n5_t[:, first // 16 : (first + count) // 16]), ACT.Copy)
                hi = ring.tile([P, HALF, 2], F32, name="hi", bufs=1)
                lo = ring.tile([P, HALF, 2], F32, name="lo", bufs=1)
                nc.vector.tensor_tensor(lo[:, 0:width, :], members[:, 0:width, 0:2], members[:, 0:width, 2:4], ALU.min)
                nc.vector.tensor_tensor(hi[:, 0:width, :], members[:, 0:width, 0:2], members[:, 0:width, 2:4], ALU.max)
                if pending:
                    finish()
                mx = ring.tile([P, HALF], F32, name="mx")
                mn = ring.tile([P, HALF], F32, name="mn")
                nc.vector.tensor_tensor(mn[:, 0:width], lo[:, 0:width, 0], lo[:, 0:width, 1], ALU.min)
                nc.vector.tensor_tensor(mx[:, 0:width], hi[:, 0:width, 0], hi[:, 0:width, 1], ALU.max)
                pending.append((m, slice(first // 4, first // 4 + width), mx, mn))
                first = first + count
        finish()
